import numpy as np
import ml_dtypes


def mxq(x, axis, fmt="e4m3"):
    dtype, down = {"e4m3": (ml_dtypes.float8_e4m3fn, 7), "e5m2": (ml_dtypes.float8_e5m2, 14)}[fmt]
    v = np.moveaxis(np.asarray(x, np.float32).astype(ml_dtypes.bfloat16).astype(np.float64), axis, -1)
    blocks = v.reshape(v.shape[:-1] + (-1, 32))
    amax = np.abs(blocks).max(-1, keepdims=True)
    byte = np.maximum(np.where(amax > 0, np.frexp(amax)[1] - 1 + 127, 0) - down, 1)
    scale = np.exp2(byte - 127.0)
    codes = (blocks / scale).astype(np.float32).astype(dtype).astype(np.float64)
    return np.moveaxis((codes * scale).reshape(v.shape), -1, axis)


WIDE = False


def mx_kscale(k, group=512):
    if not WIDE:
        return np.ones(k)
    levels = np.array([10, -10, 5, -5, 0])
    if group != 512:
        return np.exp2(np.random.permutation(np.resize(levels, k // group))).repeat(group)
    if k % 512:
        return np.exp2(np.random.permutation(np.resize(levels, k // 32))).repeat(32)
    a = np.empty((k // 512, 16))
    for p in range(k // 512):
        a[p, :8] = np.random.permutation(np.resize(levels, 8))
        for g in range(8):
            far = levels[np.abs(levels - a[p, g]) >= 10]
            a[p, g + 8] = far[np.random.randint(len(far))]
    return np.exp2(a.ravel()).repeat(32)


def f64(x):
    return np.asarray(x).astype(np.float64)


def striped(idx):
    return np.tile(np.asarray(idx).reshape(-1, 16).T, (8, 1)).astype(np.uint16)


def unstriped(offs):
    return offs[:16].T.reshape(-1).astype(np.int64)


H, KV, D, NQ, N = 2, 2, 256, 512, 512


def setup_inputs():
    n = np.random.standard_normal
    s = mx_kscale(D, 0)[:, None]
    u = mx_kscale(N)
    t = np.random.uniform(0.5, 2.0, N) * u
    v = n((KV, N, 128))
    return {
        "qT": (n((H, D, NQ)) * s * (0.70 / np.sqrt(D))).astype(np.float32),
        "kT": (n((KV, D, N)) / s).astype(np.float32),
        "t": t.reshape(N, 1).astype(np.float32),
        "v": (v / t[:, None]).astype(np.float32),
        "mask": (np.arange(N)[:, None] <= np.sort(np.random.randint(N // 4, N, NQ))[None, :]).astype(np.float32),
        "gn": np.tile(np.random.uniform(0.5, 2.0, 128), (128, 1)).astype(np.float32),
    }


def reference(qT, kT, t, v, mask, gn):
    a = mxq(f64(kT), 1, "e4m3").transpose(0, 2, 1) @ mxq(f64(qT), 1, "e4m3")
    p = np.tanh(a)
    p = p * f64(mask)
    w = p * f64(t)
    y = mxq(w, 1, "e4m3").transpose(0, 2, 1) @ mxq(f64(v), 1, "e4m3")
    y = y / 16.0
    y = y / np.sqrt(np.mean(np.square(y), -1, keepdims=True) + 1e-5) * f64(gn)[:1]
    return y

@@ -1,0 +1,278 @@
+from contextlib import ExitStack
+
+import concourse.mybir as mybir
+
+F32 = mybir.dt.float32
+BF16 = mybir.dt.bfloat16
+U32 = mybir.dt.uint32
+U8 = mybir.dt.uint8
+FP8X4 = mybir.dt.float8_e4m3fn_x4
+ACT = mybir.ActivationFunctionType
+ALU = mybir.AluOpType
+
+H, D, NQ, N, E = 2, 256, 512, 512, 128
+P = 128
+PACK = 4
+ROWS = D // PACK
+QT = 128
+TILES = NQ // QT
+FLOPS = 2 * H * NQ * N * (D + E)
+EPS = 1e-5 * 16.0 * 16.0
+K_SPLIT = 104
+
+
+def tile_rows_a_tanh_mask_onorm_kernel(tc, qT, kT, t, v, mask, gn, out):
+    nc = tc.nc
+    with ExitStack() as ctx:
+        sb = ctx.enter_context(tc.tile_pool(name="sb", bufs=1))
+        ps = ctx.enter_context(tc.psum_pool(name="ps", bufs=1))
+        ctx.enter_context(tc.manual_schedule())
+
+        def sbuf(name, shape, dtype):
+            return sb.tile(shape, dtype, name=name, align_bytes=64)
+
+        q_hbm = qT.rearrange("h (p j) q -> (h p) j q", j=PACK)
+        k_hbm = kT.rearrange("h (p j) n -> (h p) j n", j=PACK)
+        m_hbm = mask.rearrange("(s r) q -> s r q", r=PACK)
+        v_hbm = v.rearrange("h (s r) e -> s h r e", r=PACK)
+
+        chunks = [(0, 128), (128, 256), (256, 512)]
+        q_raw = [sbuf("q_raw%d" % i, [P, PACK, b - a], F32) for i, (a, b) in enumerate(chunks)]
+        m_raw = [sbuf("m_raw%d" % i, [P, PACK, b - a], F32) for i, (a, b) in enumerate(chunks)]
+        k_raw = [sbuf("k_raw%d" % i, [P, PACK, N // 2], F32) for i in range(2)]
+        v_raw = sbuf("v_raw", [P, H, PACK, E], F32)
+        t_sb = sbuf("t_sb", [P, PACK], F32)
+        gn_sb = sbuf("gn_sb", [P, E], F32)
+        warm = sbuf("warm", [P, 2], F32)
+
+        q_bf = sbuf("q_bf", [P, NQ, PACK], BF16)
+        k_bf = sbuf("k_bf", [P, PACK, P, PACK], BF16)
+        v_bf = sbuf("v_bf", [P, H, E, PACK], BF16)
+        q_codes = sbuf("q_codes", [P, NQ], U32)
+        q_scales = sbuf("q_scales", [P, NQ], U8)
+        k_codes = sbuf("k_codes", [P, N], U32)
+        k_scales = sbuf("k_scales", [P, N], U8)
+        v_codes = sbuf("v_codes", [P, H * E], U32)
+        v_scales = sbuf("v_scales", [P, H * E], U8)
+        mt = [sbuf("mt%d" % i, [P, PACK, QT], F32) for i in range(TILES)]
+        units = TILES * H
+        p_sb = [sbuf("p%d" % u, [P, PACK, QT], F32) for u in range(units)]
+        w_bf = [sbuf("w_bf%d" % u, [P, QT, PACK], BF16) for u in range(units)]
+        w_codes = [sbuf("w_codes%d" % u, [P, QT], U32) for u in range(units)]
+        w_scales = [sbuf("w_scales%d" % u, [P, QT], U8) for u in range(units)]
+        squares = sbuf("squares", [P, units, E], BF16)
+        ssq = sbuf("ssq", [P, units], F32)
+        root = sbuf("root", [P, units], F32)
+        rstd = sbuf("rstd", [P, units], F32)
+        res = [sbuf("res%d" % i, [P, H, E], F32) for i in range(TILES)]
+
+        scores = [[ps.tile([P, PACK, QT], F32, name="sc%d_%d" % (h, b)) for b in range(2)] for h in range(H)]
+        y_ps = [ps.tile([P, H, E], F32, name="y%d" % i) for i in range(TILES)]
+
+        def load_q(i):
+            nc.sync.dma_start(out=q_raw[i][:], in_=q_hbm[:, :, chunks[i][0]:chunks[i][1]])
+
+        def load_m(i):
+            nc.sync.dma_start(out=m_raw[i][:], in_=m_hbm[:, :, chunks[i][0]:chunks[i][1]])
+
+        def load_k(i):
+            nc.sync.dma_start(out=k_raw[i][:], in_=k_hbm[:, :, i * (N // 2):(i + 1) * (N // 2)])
+
+        def copy_on(engine, dst, src):
+            if engine == "V":
+                nc.vector.tensor_copy(out=dst, in_=src)
+            else:
+                nc.scalar.copy(out=dst, in_=src)
+
+        def cast_q(i, engine):
+            a, b = chunks[i]
+            copy_on(engine, q_bf[:, a:b, :].rearrange("p (c i) j -> p c j i", i=4),
+                    q_raw[i][:].rearrange("p j (c i) -> p c j i", i=4))
+
+        def cast_k(s0, s1, engine):
+            half = s0 // 64
+            src = k_raw[half][:, :, PACK * (s0 - 64 * half):PACK * (s1 - 64 * half)]
+            copy_on(engine, k_bf[:, :, s0:s1, :].rearrange("p r s j -> p s j r"),
+                    src.rearrange("p j (s r) -> p s j r", r=PACK))
+
+        def cast_v(h, engine):
+            copy_on(engine, v_bf[:, h, :, :].rearrange("p (c i) r -> p c r i", i=4),
+                    v_raw[:, h, :, :].rearrange("p r (c i) -> p c r i", i=4))
+
+        def quantize(codes, scales, src):
+            nc.vector.quantize_mx(out=codes.bitcast(FP8X4), scales=scales, in_=src)
+
+        def quant_q(i):
+            a, b = chunks[i]
+            quantize(q_codes[:, a:b], q_scales[:, a:b], q_bf[:, a:b, :].rearrange("p q j -> p (q j)"))
+
+        def quant_k(r):
+            cols = slice(r * P, (r + 1) * P)
+            quantize(k_codes[:, cols], k_scales[:, cols], k_bf[:, r, :, :].rearrange("p s j -> p (s j)"))
+
+        def quant_v():
+            quantize(v_codes[:], v_scales[:], v_bf[:].rearrange("p h e r -> p (h e r)"))
+
+        def quant_w(u):
+            quantize(w_codes[u][:], w_scales[u][:], w_bf[u][:].rearrange("p q r -> p (q r)"))
+
+        def score(i, r):
+            qc = slice(i * QT, (i + 1) * QT)
+            kc = slice(r * P, (r + 1) * P)
+            for h in range(H):
+                rows = slice(h * ROWS, (h + 1) * ROWS)
+                nc.tensor.matmul_mx(
+                    out=scores[h][i % 2][:, r, :],
+                    lhsT=k_codes[rows, kc].bitcast(FP8X4), lhsT_scale=k_scales[rows, kc],
+                    rhs=q_codes[rows, qc].bitcast(FP8X4), rhs_scale=q_scales[rows, qc],
+                    start=True, stop=True)
+
+        def scores_of(i):
+            for r in range(PACK):
+                score(i, r)
+
+        def tanh(u):
+            i, h = divmod(u, H)
+            nc.scalar.activation(out=p_sb[u][:], in_=scores[h][i % 2][:], func=ACT.Tanh)
+
+        def mask_t(i, engine):
+            c = min(i, 2)
+            a = i * QT - chunks[c][0]
+            for r in range(PACK):
+                src = m_raw[c][:, r, a:a + QT]
+                if engine == "V":
+                    nc.vector.tensor_scalar(out=mt[i][:, r, :], in0=src, scalar1=t_sb[:, r:r + 1],
+                                            scalar2=None, op0=ALU.mult)
+                else:
+                    nc.scalar.activation(out=mt[i][:, r, :], in_=src, func=ACT.Copy, scale=t_sb[:, r:r + 1])
+
+        def weigh(u):
+            nc.vector.tensor_tensor(
+                out=w_bf[u][:].rearrange("p (c i) r -> p c r i", i=4),
+                in0=p_sb[u][:].rearrange("p r (c i) -> p c r i", i=4),
+                in1=mt[u // H][:].rearrange("p r (c i) -> p c r i", i=4),
+                op=ALU.mult)
+
+        def product(u):
+            i, h = divmod(u, H)
+            ec = slice(h * E, (h + 1) * E)
+            nc.tensor.matmul_mx(
+                out=y_ps[i][:, h, :],
+                lhsT=w_codes[u][:].bitcast(FP8X4), lhsT_scale=w_scales[u][:],
+                rhs=v_codes[:, ec].bitcast(FP8X4), rhs_scale=v_scales[:, ec],
+                start=True, stop=True)
+
+        def square(u):
+            i, h = divmod(u, H)
+            nc.scalar.activation(out=squares[:, u, :], in_=y_ps[i][:, h, :], func=ACT.Square,
+                                 accum_out=ssq[:, u:u + 1])
+
+        def sqrt(a, b):
+            nc.scalar.activation(out=root[:, a:b], in_=ssq[:, a:b], func=ACT.Sqrt, scale=1.0 / E, bias=EPS)
+
+        def recip(a, b):
+            nc.vector.reciprocal(out=rstd[:, a:b], in_=root[:, a:b])
+
+        def finish(u):
+            i, h = divmod(u, H)
+            nc.vector.scalar_tensor_tensor(out=res[i][:, h, :], in0=y_ps[i][:, h, :], scalar=rstd[:, u:u + 1],
+                                           in1=gn_sb[:], op0=ALU.mult, op1=ALU.mult)
+
+        def store(i):
+            nc.sync.dma_start(out=out[:, i * QT:(i + 1) * QT, :].rearrange("h q e -> q h e"), in_=res[i][:])
+
+        load_q(0)
+        load_k(0)
+        load_k(1)
+        load_q(1)
+        load_m(0)
+        load_q(2)
+        load_m(1)
+        nc.sync.dma_start(out=v_raw[:], in_=v_hbm)
+        load_m(2)
+        nc.gpsimd.dma_start(out=t_sb[:], in_=t.rearrange("(s r) o -> s (r o)", r=PACK))
+        nc.gpsimd.dma_start(out=gn_sb[:], in_=gn)
+        nc.vector.memset(warm[:, 0:1], 0.0)
+        nc.scalar.activation(out=warm[:, 1:2], in_=warm[:, 0:1], func=ACT.Tanh)
+        cast_q(0, "S")
+        cast_k(0, 64, "V")
+        quant_q(0)
+        cast_k(64, K_SPLIT, "V")
+        cast_k(K_SPLIT, 128, "S")
+        for r in range(PACK):
+            quant_k(r)
+            score(0, r)
+        cast_q(1, "S")
+        mask_t(0, "V")
+        quant_q(1)
+        scores_of(1)
+        tanh(0)
+        tanh(1)
+        weigh(0)
+        cast_q(2, "V")
+        weigh(1)
+        quant_q(2)
+        tanh(2)
+        tanh(3)
+        scores_of(2)
+        scores_of(3)
+        mask_t(1, "S")
+        quant_w(0)
+        cast_v(0, "V")
+        quant_w(1)
+        cast_v(1, "S")
+        weigh(2)
+        quant_v()
+        tanh(4)
+        tanh(5)
+        product(0)
+        product(1)
+        weigh(3)
+        quant_w(2)
+        mask_t(2, "V")
+        quant_w(3)
+        tanh(6)
+        square(0)
+        square(1)
+        tanh(7)
+        sqrt(0, 2)
+        product(2)
+        product(3)
+        weigh(4)
+        mask_t(3, "V")
+        weigh(5)
+        quant_w(4)
+        weigh(6)
+        quant_w(5)
+        product(4)
+        product(5)
+        square(2)
+        square(3)
+        sqrt(2, 4)
+        weigh(7)
+        quant_w(6)
+        recip(0, 2)
+        quant_w(7)
+        product(6)
+        product(7)
+        square(4)
+        square(5)
+        sqrt(4, 6)
+        recip(2, 4)
+        finish(0)
+        finish(1)
+        store(0)
+        square(6)
+        square(7)
+        sqrt(6, 8)
+        finish(2)
+        finish(3)
+        store(1)
+        recip(4, 6)
+        finish(4)
+        recip(6, 8)
+        finish(5)
+        store(2)
+        finish(6)
+        finish(7)
+        store(3)

@@ -36,11 +36,11 @@ def tile_rows_a_tanh_mask_onorm_kernel(tc, qT, kT, t, v, mask, gn, out):
         m_hbm = mask.rearrange("(s r) q -> s r q", r=PACK)
         v_hbm = v.rearrange("h (s r) e -> s h r e", r=PACK)
 
-        chunks = [(0, 128), (128, 256), (256, 512)]
+        chunks = [(i * QT, (i + 1) * QT) for i in range(TILES)]
         q_raw = [sbuf("q_raw%d" % i, [P, PACK, b - a], F32) for i, (a, b) in enumerate(chunks)]
         m_raw = [sbuf("m_raw%d" % i, [P, PACK, b - a], F32) for i, (a, b) in enumerate(chunks)]
         k_raw = [sbuf("k_raw%d" % i, [P, PACK, N // 2], F32) for i in range(2)]
-        v_raw = sbuf("v_raw", [P, H, PACK, E], F32)
+        v_raw = [sbuf("v_raw%d" % h, [P, PACK, E], F32) for h in range(H)]
         t_sb = sbuf("t_sb", [P, PACK], F32)
         gn_sb = sbuf("gn_sb", [P, E], F32)
         warm = sbuf("warm", [P, 2], F32)
@@ -69,6 +69,10 @@ def tile_rows_a_tanh_mask_onorm_kernel(tc, qT, kT, t, v, mask, gn, out):
         scores = [[ps.tile([P, PACK, QT], F32, name="sc%d_%d" % (h, b)) for b in range(2)] for h in range(H)]
         y_ps = [ps.tile([P, H, E], F32, name="y%d" % i) for i in range(TILES)]
 
+        def y_of(u):
+            bank, slot = [(0, 0), (0, 1), (1, 0), (1, 1), (2, 0), (3, 0), (3, 1), (2, 1)][u]
+            return y_ps[bank][:, slot, :]
+
         def load_q(i):
             nc.sync.dma_start(out=q_raw[i][:], in_=q_hbm[:, :, chunks[i][0]:chunks[i][1]])
 
@@ -77,6 +81,9 @@ def tile_rows_a_tanh_mask_onorm_kernel(tc, qT, kT, t, v, mask, gn, out):
 
         def load_k(i):
             nc.sync.dma_start(out=k_raw[i][:], in_=k_hbm[:, :, i * (N // 2):(i + 1) * (N // 2)])
+
+        def load_v(h):
+            nc.sync.dma_start(out=v_raw[h][:], in_=v_hbm[:, h, :, :])
 
         def copy_on(engine, dst, src):
             if engine == "V":
@@ -92,12 +99,12 @@ def tile_rows_a_tanh_mask_onorm_kernel(tc, qT, kT, t, v, mask, gn, out):
         def cast_k(s0, s1, engine):
             half = s0 // 64
             src = k_raw[half][:, :, PACK * (s0 - 64 * half):PACK * (s1 - 64 * half)]
-            copy_on(engine, k_bf[:, :, s0:s1, :].rearrange("p r s j -> p s j r"),
-                    src.rearrange("p j (s r) -> p s j r", r=PACK))
+            copy_on(engine, k_bf[:, :, s0:s1, :].rearrange("p (a b) s j -> p s a j b", b=2),
+                    src.rearrange("p j (s a b) -> p s a j b", a=2, b=2))
 
         def cast_v(h, engine):
             copy_on(engine, v_bf[:, h, :, :].rearrange("p (c i) r -> p c r i", i=4),
-                    v_raw[:, h, :, :].rearrange("p r (c i) -> p c r i", i=4))
+                    v_raw[h][:].rearrange("p r (c i) -> p c r i", i=4))
 
         def quantize(codes, scales, src):
             nc.vector.quantize_mx(out=codes.bitcast(FP8X4), scales=scales, in_=src)
@@ -106,40 +113,40 @@ def tile_rows_a_tanh_mask_onorm_kernel(tc, qT, kT, t, v, mask, gn, out):
             a, b = chunks[i]
             quantize(q_codes[:, a:b], q_scales[:, a:b], q_bf[:, a:b, :].rearrange("p q j -> p (q j)"))
 
-        def quant_k(r):
-            cols = slice(r * P, (r + 1) * P)
-            quantize(k_codes[:, cols], k_scales[:, cols], k_bf[:, r, :, :].rearrange("p s j -> p (s j)"))
+        def quant_k(r, half):
+            cols = slice(r * P + half * 64, r * P + (half + 1) * 64)
+            quantize(k_codes[:, cols], k_scales[:, cols],
+                     k_bf[:, r, half * 64:(half + 1) * 64, :].rearrange("p s j -> p (s j)"))
 
-        def quant_v():
-            quantize(v_codes[:], v_scales[:], v_bf[:].rearrange("p h e r -> p (h e r)"))
+        def quant_v(h):
+            cols = slice(h * E, (h + 1) * E)
+            quantize(v_codes[:, cols], v_scales[:, cols], v_bf[:, h, :, :].rearrange("p e r -> p (e r)"))
 
         def quant_w(u):
             quantize(w_codes[u][:], w_scales[u][:], w_bf[u][:].rearrange("p q r -> p (q r)"))
 
-        def score(i, r):
+        def score(u, r):
+            i, h = divmod(u, H)
             qc = slice(i * QT, (i + 1) * QT)
             kc = slice(r * P, (r + 1) * P)
-            for h in range(H):
-                rows = slice(h * ROWS, (h + 1) * ROWS)
-                nc.tensor.matmul_mx(
-                    out=scores[h][i % 2][:, r, :],
-                    lhsT=k_codes[rows, kc].bitcast(FP8X4), lhsT_scale=k_scales[rows, kc],
-                    rhs=q_codes[rows, qc].bitcast(FP8X4), rhs_scale=q_scales[rows, qc],
-                    start=True, stop=True)
+            rows = slice(h * ROWS, (h + 1) * ROWS)
+            nc.tensor.matmul_mx(
+                out=scores[h][i % 2][:, r, :],
+                lhsT=k_codes[rows, kc].bitcast(FP8X4), lhsT_scale=k_scales[rows, kc],
+                rhs=q_codes[rows, qc].bitcast(FP8X4), rhs_scale=q_scales[rows, qc],
+                start=True, stop=True)
 
-        def scores_of(i):
+        def scores_of(u):
             for r in range(PACK):
-                score(i, r)
+                score(u, r)
 
         def tanh(u):
             i, h = divmod(u, H)
             nc.scalar.activation(out=p_sb[u][:], in_=scores[h][i % 2][:], func=ACT.Tanh)
 
         def mask_t(i, engine):
-            c = min(i, 2)
-            a = i * QT - chunks[c][0]
             for r in range(PACK):
-                src = m_raw[c][:, r, a:a + QT]
+                src = m_raw[i][:, r, :]
                 if engine == "V":
                     nc.vector.tensor_scalar(out=mt[i][:, r, :], in0=src, scalar1=t_sb[:, r:r + 1],
                                             scalar2=None, op0=ALU.mult)
@@ -148,130 +155,153 @@ def tile_rows_a_tanh_mask_onorm_kernel(tc, qT, kT, t, v, mask, gn, out):
 
         def weigh(u):
             nc.vector.tensor_tensor(
-                out=w_bf[u][:].rearrange("p (c i) r -> p c r i", i=4),
-                in0=p_sb[u][:].rearrange("p r (c i) -> p c r i", i=4),
-                in1=mt[u // H][:].rearrange("p r (c i) -> p c r i", i=4),
+                out=w_bf[u][:].rearrange("p (c i) r -> p c r i", i=2),
+                in0=p_sb[u][:].rearrange("p r (c i) -> p c r i", i=2),
+                in1=mt[u // H][:].rearrange("p r (c i) -> p c r i", i=2),
                 op=ALU.mult)
 
         def product(u):
             i, h = divmod(u, H)
             ec = slice(h * E, (h + 1) * E)
             nc.tensor.matmul_mx(
-                out=y_ps[i][:, h, :],
+                out=y_of(u),
                 lhsT=w_codes[u][:].bitcast(FP8X4), lhsT_scale=w_scales[u][:],
                 rhs=v_codes[:, ec].bitcast(FP8X4), rhs_scale=v_scales[:, ec],
                 start=True, stop=True)
 
         def square(u):
             i, h = divmod(u, H)
-            nc.scalar.activation(out=squares[:, u, :], in_=y_ps[i][:, h, :], func=ACT.Square,
+            nc.scalar.activation(out=squares[:, u, :], in_=y_of(u), func=ACT.Square,
                                  accum_out=ssq[:, u:u + 1])
 
         def sqrt(a, b):
             nc.scalar.activation(out=root[:, a:b], in_=ssq[:, a:b], func=ACT.Sqrt, scale=1.0 / E, bias=EPS)
+
+        def rsqrt(a, b):
+            nc.scalar.activation(out=rstd[:, a:b], in_=ssq[:, a:b], func=ACT.Abs_reciprocal_sqrt, scale=1.0 / E, bias=EPS)
 
         def recip(a, b):
             nc.vector.reciprocal(out=rstd[:, a:b], in_=root[:, a:b])
 
         def finish(u):
             i, h = divmod(u, H)
-            nc.vector.scalar_tensor_tensor(out=res[i][:, h, :], in0=y_ps[i][:, h, :], scalar=rstd[:, u:u + 1],
+            nc.vector.scalar_tensor_tensor(out=res[i][:, h, :], in0=y_of(u), scalar=rstd[:, u:u + 1],
                                            in1=gn_sb[:], op0=ALU.mult, op1=ALU.mult)
 
         def store(i):
             nc.sync.dma_start(out=out[:, i * QT:(i + 1) * QT, :].rearrange("h q e -> q h e"), in_=res[i][:])
 
-        load_q(0)
         load_k(0)
+        load_q(0)
         load_k(1)
         load_q(1)
-        load_m(0)
         load_q(2)
+        nc.sync.dma_start(out=t_sb[:], in_=t.rearrange("(s r) o -> s (r o)", r=PACK))
+        load_m(0)
         load_m(1)
-        nc.sync.dma_start(out=v_raw[:], in_=v_hbm)
+        load_q(3)
+        load_v(0)
         load_m(2)
-        nc.gpsimd.dma_start(out=t_sb[:], in_=t.rearrange("(s r) o -> s (r o)", r=PACK))
-        nc.gpsimd.dma_start(out=gn_sb[:], in_=gn)
+        load_v(1)
+        load_m(3)
+        nc.sync.dma_start(out=gn_sb[:], in_=gn)
         nc.vector.memset(warm[:, 0:1], 0.0)
         nc.scalar.activation(out=warm[:, 1:2], in_=warm[:, 0:1], func=ACT.Tanh)
-        cast_q(0, "S")
         cast_k(0, 64, "V")
+        cast_q(0, "S")
+        quant_k(0, 0)
+        quant_k(1, 0)
+        quant_k(2, 0)
+        quant_k(3, 0)
         quant_q(0)
-        cast_k(64, K_SPLIT, "V")
         cast_k(K_SPLIT, 128, "S")
-        for r in range(PACK):
-            quant_k(r)
-            score(0, r)
+        cast_k(64, K_SPLIT, "V")
         cast_q(1, "S")
-        mask_t(0, "V")
+        quant_k(0, 1)
+        quant_k(1, 1)
+        quant_k(2, 1)
+        quant_k(3, 1)
+        score(0, 0)
+        score(0, 1)
+        cast_q(2, "S")
+        score(0, 2)
+        score(0, 3)
         quant_q(1)
-        scores_of(1)
+        score(1, 0)
+        score(1, 1)
+        mask_t(0, "V")
+        score(1, 2)
         tanh(0)
-        tanh(1)
-        weigh(0)
-        cast_q(2, "V")
-        weigh(1)
-        quant_q(2)
-        tanh(2)
-        tanh(3)
+        score(1, 3)
         scores_of(2)
+        quant_q(2)
+        mask_t(1, "V")
+        tanh(1)
         scores_of(3)
-        mask_t(1, "S")
-        quant_w(0)
+        weigh(0)
+        tanh(2)
+        scores_of(4)
+        cast_q(3, "V")
         cast_v(0, "V")
-        quant_w(1)
-        cast_v(1, "S")
-        weigh(2)
-        quant_v()
+        tanh(3)
+        scores_of(5)
+        weigh(1)
         tanh(4)
+        quant_q(3)
+        weigh(2)
+        mask_t(2, "S")
+        scores_of(6)
+        cast_v(1, "V")
         tanh(5)
-        product(0)
-        product(1)
+        scores_of(7)
+        quant_v(0)
         weigh(3)
-        quant_w(2)
-        mask_t(2, "V")
-        quant_w(3)
         tanh(6)
-        square(0)
-        square(1)
-        tanh(7)
-        sqrt(0, 2)
-        product(2)
-        product(3)
-        weigh(4)
+        quant_w(0)
         mask_t(3, "V")
+        tanh(7)
+        product(0)
+        quant_w(1)
+        quant_v(1)
+        product(1)
+        weigh(4)
+        square(0)
+        nc.scalar.activation(out=warm[:, 0:1], in_=warm[:, 1:2], func=ACT.Abs_reciprocal_sqrt, bias=1.0)
         weigh(5)
+        quant_w(2)
+        quant_w(3)
         quant_w(4)
-        weigh(6)
+        product(2)
         quant_w(5)
+        product(3)
+        weigh(6)
         product(4)
         product(5)
+        square(1)
         square(2)
-        square(3)
-        sqrt(2, 4)
         weigh(7)
+        square(3)
+        square(4)
+        rsqrt(0, 2)
         quant_w(6)
-        recip(0, 2)
+        square(5)
+        rsqrt(2, 4)
         quant_w(7)
         product(6)
-        product(7)
-        square(4)
-        square(5)
-        sqrt(4, 6)
-        recip(2, 4)
         finish(0)
+        rsqrt(4, 6)
         finish(1)
-        store(0)
-        square(6)
-        square(7)
-        sqrt(6, 8)
+        product(7)
         finish(2)
+        square(6)
         finish(3)
-        store(1)
-        recip(4, 6)
+        store(0)
         finish(4)
-        recip(6, 8)
+        square(7)
+        rsqrt(6, 7)
         finish(5)
+        store(1)
+        rsqrt(7, 8)
         store(2)
         finish(6)
         finish(7)

@@ -36,10 +36,17 @@ def tile_rows_a_tanh_mask_onorm_kernel(tc, qT, kT, t, v, mask, gn, out):
         m_hbm = mask.rearrange("(s r) q -> s r q", r=PACK)
         v_hbm = v.rearrange("h (s r) e -> s h r e", r=PACK)
 
-        chunks = [(i * QT, (i + 1) * QT) for i in range(TILES)]
-        q_raw = [sbuf("q_raw%d" % i, [P, PACK, b - a], F32) for i, (a, b) in enumerate(chunks)]
-        m_raw = [sbuf("m_raw%d" % i, [P, PACK, b - a], F32) for i, (a, b) in enumerate(chunks)]
-        k_raw = [sbuf("k_raw%d" % i, [P, PACK, N // 2], F32) for i in range(2)]
+        q_chunks = [[0],[1],[2,3]]
+        m_chunks = [[0,1],[2,3]]
+        k_parts = 1
+        k_span = P // k_parts
+        q_raw = [sbuf("q_raw%d" % c[0], [P, PACK, QT * len(c)], F32) for c in q_chunks]
+        m_raw = [sbuf("m_raw%d" % c[0], [P, PACK, QT * len(c)], F32) for c in m_chunks]
+        k_raw = [sbuf("k_raw%d" % i, [P, PACK, N // k_parts], F32) for i in range(k_parts)]
+
+        def place(chunks, i):
+            n = [i in c for c in chunks].index(True)
+            return n, (i - chunks[n][0]) * QT
         v_raw = [sbuf("v_raw%d" % h, [P, PACK, E], F32) for h in range(H)]
         t_sb = sbuf("t_sb", [P, PACK], F32)
         gn_sb = sbuf("gn_sb", [P, E], F32)
@@ -54,7 +61,7 @@ def tile_rows_a_tanh_mask_onorm_kernel(tc, qT, kT, t, v, mask, gn, out):
         k_scales = sbuf("k_scales", [P, N], U8)
         v_codes = sbuf("v_codes", [P, H * E], U32)
         v_scales = sbuf("v_scales", [P, H * E], U8)
-        mt = [sbuf("mt%d" % i, [P, PACK, QT], F32) for i in range(TILES)]
+        mt = [sbuf("mt%d" % c[0], [P, PACK, QT * len(c)], F32) for c in m_chunks]
         units = TILES * H
         p_sb = [sbuf("p%d" % u, [P, PACK, QT], F32) for u in range(units)]
         w_bf = [sbuf("w_bf%d" % u, [P, QT, PACK], BF16) for u in range(units)]
@@ -74,13 +81,15 @@ def tile_rows_a_tanh_mask_onorm_kernel(tc, qT, kT, t, v, mask, gn, out):
             return y_ps[bank][:, slot, :]
 
         def load_q(i):
-            nc.sync.dma_start(out=q_raw[i][:], in_=q_hbm[:, :, chunks[i][0]:chunks[i][1]])
+            n = place(q_chunks, i)[0]
+            nc.sync.dma_start(out=q_raw[n][:], in_=q_hbm[:, :, i * QT:(i + len(q_chunks[n])) * QT])
 
         def load_m(i):
-            nc.sync.dma_start(out=m_raw[i][:], in_=m_hbm[:, :, chunks[i][0]:chunks[i][1]])
+            n = place(m_chunks, i)[0]
+            nc.sync.dma_start(out=m_raw[n][:], in_=m_hbm[:, :, i * QT:(i + len(m_chunks[n])) * QT])
 
         def load_k(i):
-            nc.sync.dma_start(out=k_raw[i][:], in_=k_hbm[:, :, i * (N // 2):(i + 1) * (N // 2)])
+            nc.sync.dma_start(out=k_raw[i][:], in_=k_hbm[:, :, i * (N // k_parts):(i + 1) * (N // k_parts)])
 
         def load_v(h):
             nc.sync.dma_start(out=v_raw[h][:], in_=v_hbm[:, h, :, :])
@@ -92,13 +101,13 @@ def tile_rows_a_tanh_mask_onorm_kernel(tc, qT, kT, t, v, mask, gn, out):
                 nc.scalar.copy(out=dst, in_=src)
 
         def cast_q(i, engine):
-            a, b = chunks[i]
-            copy_on(engine, q_bf[:, a:b, :].rearrange("p (c i) j -> p c j i", i=4),
-                    q_raw[i][:].rearrange("p j (c i) -> p c j i", i=4))
+            n, a = place(q_chunks, i)
+            copy_on(engine, q_bf[:, i * QT:(i + 1) * QT, :].rearrange("p (c i) j -> p c j i", i=4),
+                    q_raw[n][:, :, a:a + QT].rearrange("p j (c i) -> p c j i", i=4))
 
         def cast_k(s0, s1, engine):
-            half = s0 // 64
-            src = k_raw[half][:, :, PACK * (s0 - 64 * half):PACK * (s1 - 64 * half)]
+            part = s0 // k_span
+            src = k_raw[part][:, :, PACK * (s0 - k_span * part):PACK * (s1 - k_span * part)]
             copy_on(engine, k_bf[:, :, s0:s1, :].rearrange("p (a b) s j -> p s a j b", b=2),
                     src.rearrange("p j (s a b) -> p s a j b", a=2, b=2))
 
@@ -110,13 +119,13 @@ def tile_rows_a_tanh_mask_onorm_kernel(tc, qT, kT, t, v, mask, gn, out):
             nc.vector.quantize_mx(out=codes.bitcast(FP8X4), scales=scales, in_=src)
 
         def quant_q(i):
-            a, b = chunks[i]
+            a, b = i * QT, (i + 1) * QT
             quantize(q_codes[:, a:b], q_scales[:, a:b], q_bf[:, a:b, :].rearrange("p q j -> p (q j)"))
 
-        def quant_k(r, half):
-            cols = slice(r * P + half * 64, r * P + (half + 1) * 64)
+        def quant_k(r, part):
+            cols = slice(r * P + part * k_span, r * P + (part + 1) * k_span)
             quantize(k_codes[:, cols], k_scales[:, cols],
-                     k_bf[:, r, half * 64:(half + 1) * 64, :].rearrange("p s j -> p (s j)"))
+                     k_bf[:, r, part * k_span:(part + 1) * k_span, :].rearrange("p s j -> p (s j)"))
 
         def quant_v(h):
             cols = slice(h * E, (h + 1) * E)
@@ -136,15 +145,20 @@ def tile_rows_a_tanh_mask_onorm_kernel(tc, qT, kT, t, v, mask, gn, out):
                 rhs=q_codes[rows, qc].bitcast(FP8X4), rhs_scale=q_scales[rows, qc],
                 start=True, stop=True)
 
-        def scores_of(u):
+        def pair(i, r):
+            for h in range(H):
+                score(H * i + h, r)
+
+        def scores_of(i):
             for r in range(PACK):
-                score(u, r)
+                pair(i, r)
 
         def tanh(u):
             i, h = divmod(u, H)
             nc.scalar.activation(out=p_sb[u][:], in_=scores[h][i % 2][:], func=ACT.Tanh)
 
-        def mask_t(i, engine):
+        def mask_t(first, engine):
+            i = place(m_chunks, first)[0]
             for r in range(PACK):
                 src = m_raw[i][:, r, :]
                 if engine == "V":
@@ -154,10 +168,11 @@ def tile_rows_a_tanh_mask_onorm_kernel(tc, qT, kT, t, v, mask, gn, out):
                     nc.scalar.activation(out=mt[i][:, r, :], in_=src, func=ACT.Copy, scale=t_sb[:, r:r + 1])
 
         def weigh(u):
+            n, a = place(m_chunks, u // H)
             nc.vector.tensor_tensor(
                 out=w_bf[u][:].rearrange("p (c i) r -> p c r i", i=2),
                 in0=p_sb[u][:].rearrange("p r (c i) -> p c r i", i=2),
-                in1=mt[u // H][:].rearrange("p r (c i) -> p c r i", i=2),
+                in1=mt[n][:, :, a:a + QT].rearrange("p r (c i) -> p c r i", i=2),
                 op=ALU.mult)
 
         def product(u):
@@ -191,118 +206,100 @@ def tile_rows_a_tanh_mask_onorm_kernel(tc, qT, kT, t, v, mask, gn, out):
         def store(i):
             nc.sync.dma_start(out=out[:, i * QT:(i + 1) * QT, :].rearrange("h q e -> q h e"), in_=res[i][:])
 
+        nc.scalar.dma_start(out=t_sb[:], in_=t.rearrange("(s r) o -> s (r o)", r=PACK))
         load_k(0)
         load_q(0)
-        load_k(1)
         load_q(1)
-        load_q(2)
-        nc.sync.dma_start(out=t_sb[:], in_=t.rearrange("(s r) o -> s (r o)", r=PACK))
         load_m(0)
-        load_m(1)
-        load_q(3)
+        load_q(2)
         load_v(0)
         load_m(2)
         load_v(1)
-        load_m(3)
         nc.sync.dma_start(out=gn_sb[:], in_=gn)
         nc.vector.memset(warm[:, 0:1], 0.0)
         nc.scalar.activation(out=warm[:, 1:2], in_=warm[:, 0:1], func=ACT.Tanh)
-        cast_k(0, 64, "V")
-        cast_q(0, "S")
+        cast_k(0, 84, "V")
+        cast_k(84, 128, "S")
+        cast_q(0, "V")
         quant_k(0, 0)
+        quant_q(0)
         quant_k(1, 0)
         quant_k(2, 0)
+        pair(0, 0)
+        cast_q(1, "V")
+        pair(0, 1)
         quant_k(3, 0)
-        quant_q(0)
-        cast_k(K_SPLIT, 128, "S")
-        cast_k(64, K_SPLIT, "V")
-        cast_q(1, "S")
-        quant_k(0, 1)
-        quant_k(1, 1)
-        quant_k(2, 1)
-        quant_k(3, 1)
-        score(0, 0)
-        score(0, 1)
-        cast_q(2, "S")
-        score(0, 2)
-        score(0, 3)
+        pair(0, 2)
         quant_q(1)
-        score(1, 0)
-        score(1, 1)
+        pair(0, 3)
+        scores_of(1)
         mask_t(0, "V")
-        score(1, 2)
         tanh(0)
-        score(1, 3)
-        scores_of(2)
-        quant_q(2)
-        mask_t(1, "V")
         tanh(1)
-        scores_of(3)
         weigh(0)
+        cast_q(3, "S")
+        cast_q(2, "V")
+        quant_w(0)
         tanh(2)
-        scores_of(4)
-        cast_q(3, "V")
-        cast_v(0, "V")
-        tanh(3)
-        scores_of(5)
+        quant_q(2)
         weigh(1)
-        tanh(4)
+        scores_of(2)
+        tanh(3)
         quant_q(3)
         weigh(2)
-        mask_t(2, "S")
-        scores_of(6)
-        cast_v(1, "V")
-        tanh(5)
-        scores_of(7)
-        quant_v(0)
+        cast_v(0, "S")
         weigh(3)
-        tanh(6)
-        quant_w(0)
-        mask_t(3, "V")
-        tanh(7)
-        product(0)
+        scores_of(3)
+        tanh(4)
+        quant_v(0)
         quant_w(1)
-        quant_v(1)
-        product(1)
-        weigh(4)
-        square(0)
-        nc.scalar.activation(out=warm[:, 0:1], in_=warm[:, 1:2], func=ACT.Abs_reciprocal_sqrt, bias=1.0)
-        weigh(5)
         quant_w(2)
+        tanh(5)
+        mask_t(2, "V")
+        product(0)
+        tanh(6)
+        cast_v(1, "V")
+        weigh(4)
+        tanh(7)
+        quant_v(1)
+        square(0)
         quant_w(3)
-        quant_w(4)
+        weigh(5)
+        nc.scalar.activation(out=warm[:, 0:1], in_=warm[:, 1:2], func=ACT.Abs_reciprocal_sqrt, bias=1.0)
+        product(1)
         product(2)
-        quant_w(5)
         product(3)
         weigh(6)
+        quant_w(4)
+        quant_w(5)
+        weigh(7)
         product(4)
         product(5)
         square(1)
-        square(2)
-        weigh(7)
-        square(3)
-        square(4)
-        rsqrt(0, 2)
         quant_w(6)
-        square(5)
-        rsqrt(2, 4)
+        square(2)
         quant_w(7)
+        square(3)
         product(6)
-        finish(0)
-        rsqrt(4, 6)
-        finish(1)
+        rsqrt(0, 2)
+        square(4)
         product(7)
-        finish(2)
+        rsqrt(2, 4)
+        finish(0)
+        square(5)
+        finish(1)
         square(6)
+        finish(2)
+        rsqrt(4, 6)
         finish(3)
         store(0)
-        finish(4)
         square(7)
         rsqrt(6, 7)
-        finish(5)
+        finish(4)
         store(1)
+        finish(5)
         rsqrt(7, 8)
-        store(2)
         finish(6)
         finish(7)
+        store(2)
         store(3)

@@ -37,7 +37,7 @@ def tile_rows_a_tanh_mask_onorm_kernel(tc, qT, kT, t, v, mask, gn, out):
         v_hbm = v.rearrange("h (s r) e -> s h r e", r=PACK)
 
         q_chunks = [[0],[1],[2,3]]
-        m_chunks = [[0,1],[2,3]]
+        m_chunks = [[0],[1],[2,3]]
         k_parts = 1
         k_span = P // k_parts
         q_raw = [sbuf("q_raw%d" % c[0], [P, PACK, QT * len(c)], F32) for c in q_chunks]
@@ -203,6 +203,10 @@ def tile_rows_a_tanh_mask_onorm_kernel(tc, qT, kT, t, v, mask, gn, out):
             nc.vector.scalar_tensor_tensor(out=res[i][:, h, :], in0=y_of(u), scalar=rstd[:, u:u + 1],
                                            in1=gn_sb[:], op0=ALU.mult, op1=ALU.mult)
 
+        def store_unit(u):
+            i, h = divmod(u, H)
+            nc.sync.dma_start(out=out[h, i * QT:(i + 1) * QT, :], in_=res[i][:, h, :])
+
         def store(i):
             nc.sync.dma_start(out=out[:, i * QT:(i + 1) * QT, :].rearrange("h q e -> q h e"), in_=res[i][:])
 
@@ -210,11 +214,12 @@ def tile_rows_a_tanh_mask_onorm_kernel(tc, qT, kT, t, v, mask, gn, out):
         load_k(0)
         load_q(0)
         load_q(1)
-        load_m(0)
         load_q(2)
+        load_m(0)
         load_v(0)
-        load_m(2)
+        load_m(1)
         load_v(1)
+        load_m(2)
         nc.sync.dma_start(out=gn_sb[:], in_=gn)
         nc.vector.memset(warm[:, 0:1], 0.0)
         nc.scalar.activation(out=warm[:, 1:2], in_=warm[:, 0:1], func=ACT.Tanh)
@@ -223,83 +228,85 @@ def tile_rows_a_tanh_mask_onorm_kernel(tc, qT, kT, t, v, mask, gn, out):
         cast_q(0, "V")
         quant_k(0, 0)
         quant_q(0)
+        cast_q(1, "S")
         quant_k(1, 0)
         quant_k(2, 0)
         pair(0, 0)
-        cast_q(1, "V")
         pair(0, 1)
         quant_k(3, 0)
-        pair(0, 2)
         quant_q(1)
+        pair(0, 2)
+        cast_q(2, "V")
+        cast_q(3, "S")
         pair(0, 3)
         scores_of(1)
+        quant_q(2)
         mask_t(0, "V")
         tanh(0)
-        tanh(1)
-        weigh(0)
-        cast_q(3, "S")
-        cast_q(2, "V")
-        quant_w(0)
-        tanh(2)
-        quant_q(2)
-        weigh(1)
-        scores_of(2)
-        tanh(3)
         quant_q(3)
+        tanh(1)
+        cast_v(0, "V")
+        weigh(0)
+        tanh(2)
+        scores_of(2)
+        mask_t(1, "V")
+        tanh(3)
+        weigh(1)
+        cast_v(1, "S")
         weigh(2)
-        cast_v(0, "S")
-        weigh(3)
         scores_of(3)
         tanh(4)
         quant_v(0)
-        quant_w(1)
-        quant_w(2)
-        tanh(5)
+        quant_w(0)
         mask_t(2, "V")
+        tanh(5)
         product(0)
-        tanh(6)
-        cast_v(1, "V")
-        weigh(4)
-        tanh(7)
         quant_v(1)
+        tanh(6)
+        weigh(3)
+        tanh(7)
+        quant_w(1)
+        weigh(4)
         square(0)
-        quant_w(3)
-        weigh(5)
         nc.scalar.activation(out=warm[:, 0:1], in_=warm[:, 1:2], func=ACT.Abs_reciprocal_sqrt, bias=1.0)
         product(1)
-        product(2)
-        product(3)
-        weigh(6)
+        quant_w(2)
+        quant_w(3)
         quant_w(4)
+        product(2)
+        weigh(5)
+        product(3)
+        product(4)
+        weigh(6)
         quant_w(5)
         weigh(7)
-        product(4)
-        product(5)
         square(1)
-        quant_w(6)
+        product(5)
         square(2)
-        quant_w(7)
         square(3)
-        product(6)
-        rsqrt(0, 2)
+        quant_w(6)
         square(4)
-        product(7)
+        quant_w(7)
+        rsqrt(0, 2)
+        square(5)
+        product(6)
         rsqrt(2, 4)
         finish(0)
-        square(5)
+        product(7)
         finish(1)
-        square(6)
-        finish(2)
         rsqrt(4, 6)
+        finish(2)
+        square(6)
         finish(3)
         store(0)
         square(7)
-        rsqrt(6, 7)
         finish(4)
-        store(1)
+        rsqrt(6, 7)
         finish(5)
+        store(1)
         rsqrt(7, 8)
-        finish(6)
-        finish(7)
         store(2)
-        store(3)
+        finish(6)
+        store_unit(6)
+        finish(7)
+        store_unit(7)

@@ -11,14 +11,20 @@ ACT = mybir.ActivationFunctionType
 ALU = mybir.AluOpType
 
 H, D, NQ, N, E = 2, 256, 512, 512, 128
+FLOPS = 2 * H * NQ * N * (D + E)
+
 P = 128
 PACK = 4
 ROWS = D // PACK
 QT = 128
 TILES = NQ // QT
-FLOPS = 2 * H * NQ * N * (D + E)
+UNITS = TILES * H
 EPS = 1e-5 * 16.0 * 16.0
-K_SPLIT = 104
+LOADS = [[0], [1], [2, 3]]
+K_VECTOR = 84
+Q_VECTOR = 80
+Y_PLACE = [(0, 0), (0, 1), (0, 2), (1, 0), (1, 1), (1, 2), (2, 0), (3, 0)]
+Y_BANKS, Y_SLOTS = 4, 3
 
 
 def tile_rows_a_tanh_mask_onorm_kernel(tc, qT, kT, t, v, mask, gn, out):
@@ -36,21 +42,14 @@ def tile_rows_a_tanh_mask_onorm_kernel(tc, qT, kT, t, v, mask, gn, out):
         m_hbm = mask.rearrange("(s r) q -> s r q", r=PACK)
         v_hbm = v.rearrange("h (s r) e -> s h r e", r=PACK)
 
-        q_chunks = [[0],[1],[2,3]]
-        m_chunks = [[0],[1],[2,3]]
-        k_parts = 1
-        k_span = P // k_parts
-        q_raw = [sbuf("q_raw%d" % c[0], [P, PACK, QT * len(c)], F32) for c in q_chunks]
-        m_raw = [sbuf("m_raw%d" % c[0], [P, PACK, QT * len(c)], F32) for c in m_chunks]
-        k_raw = [sbuf("k_raw%d" % i, [P, PACK, N // k_parts], F32) for i in range(k_parts)]
-
-        def place(chunks, i):
-            n = [i in c for c in chunks].index(True)
-            return n, (i - chunks[n][0]) * QT
+        q_raw = [sbuf("q_raw%d" % c[0], [P, PACK, QT * len(c)], F32) for c in LOADS]
+        m_raw = [sbuf("m_raw%d" % c[0], [P, PACK, QT * len(c)], F32) for c in LOADS]
+        k_raw = sbuf("k_raw", [P, PACK, N], F32)
         v_raw = [sbuf("v_raw%d" % h, [P, PACK, E], F32) for h in range(H)]
         t_sb = sbuf("t_sb", [P, PACK], F32)
         gn_sb = sbuf("gn_sb", [P, E], F32)
-        warm = sbuf("warm", [P, 2], F32)
+        zero = sbuf("zero", [P, 1], F32)
+        eps = sbuf("eps", [P, 1], F32)
 
         q_bf = sbuf("q_bf", [P, NQ, PACK], BF16)
         k_bf = sbuf("k_bf", [P, PACK, P, PACK], BF16)
@@ -61,35 +60,30 @@ def tile_rows_a_tanh_mask_onorm_kernel(tc, qT, kT, t, v, mask, gn, out):
         k_scales = sbuf("k_scales", [P, N], U8)
         v_codes = sbuf("v_codes", [P, H * E], U32)
         v_scales = sbuf("v_scales", [P, H * E], U8)
-        mt = [sbuf("mt%d" % c[0], [P, PACK, QT * len(c)], F32) for c in m_chunks]
-        units = TILES * H
-        p_sb = [sbuf("p%d" % u, [P, PACK, QT], F32) for u in range(units)]
-        w_bf = [sbuf("w_bf%d" % u, [P, QT, PACK], BF16) for u in range(units)]
-        w_codes = [sbuf("w_codes%d" % u, [P, QT], U32) for u in range(units)]
-        w_scales = [sbuf("w_scales%d" % u, [P, QT], U8) for u in range(units)]
-        squares = sbuf("squares", [P, units, E], BF16)
-        ssq = sbuf("ssq", [P, units], F32)
-        root = sbuf("root", [P, units], F32)
-        rstd = sbuf("rstd", [P, units], F32)
+        mt = [sbuf("mt%d" % c[0], [P, PACK, QT * len(c)], F32) for c in LOADS]
+        p_sb = [sbuf("p%d" % u, [P, PACK, QT], F32) for u in range(UNITS)]
+        w_bf = [sbuf("w_bf%d" % u, [P, QT, PACK], BF16) for u in range(UNITS)]
+        w_codes = [sbuf("w_codes%d" % u, [P, QT], U32) for u in range(UNITS)]
+        w_scales = [sbuf("w_scales%d" % u, [P, QT], U8) for u in range(UNITS)]
+        squares = sbuf("squares", [P, UNITS, E], BF16)
+        ssq = sbuf("ssq", [P, UNITS], F32)
+        rstd = sbuf("rstd", [P, UNITS], F32)
         res = [sbuf("res%d" % i, [P, H, E], F32) for i in range(TILES)]
 
         scores = [[ps.tile([P, PACK, QT], F32, name="sc%d_%d" % (h, b)) for b in range(2)] for h in range(H)]
-        y_ps = [ps.tile([P, H, E], F32, name="y%d" % i) for i in range(TILES)]
+        y_ps = [ps.tile([P, Y_SLOTS, E], F32, name="y%d" % b) for b in range(Y_BANKS)]
 
         def y_of(u):
-            bank, slot = [(0, 0), (0, 1), (1, 0), (1, 1), (2, 0), (3, 0), (3, 1), (2, 1)][u]
+            bank, slot = Y_PLACE[u]
             return y_ps[bank][:, slot, :]
 
-        def load_q(i):
-            n = place(q_chunks, i)[0]
-            nc.sync.dma_start(out=q_raw[n][:], in_=q_hbm[:, :, i * QT:(i + len(q_chunks[n])) * QT])
+        def place(i):
+            n = [i in c for c in LOADS].index(True)
+            return n, (i - LOADS[n][0]) * QT
 
-        def load_m(i):
-            n = place(m_chunks, i)[0]
-            nc.sync.dma_start(out=m_raw[n][:], in_=m_hbm[:, :, i * QT:(i + len(m_chunks[n])) * QT])
-
-        def load_k(i):
-            nc.sync.dma_start(out=k_raw[i][:], in_=k_hbm[:, :, i * (N // k_parts):(i + 1) * (N // k_parts)])
+        def load_columns(tiles, hbm, n):
+            first = LOADS[n][0] * QT
+            nc.sync.dma_start(out=tiles[n][:], in_=hbm[:, :, first:first + len(LOADS[n]) * QT])
 
         def load_v(h):
             nc.sync.dma_start(out=v_raw[h][:], in_=v_hbm[:, h, :, :])
@@ -100,18 +94,16 @@ def tile_rows_a_tanh_mask_onorm_kernel(tc, qT, kT, t, v, mask, gn, out):
             else:
                 nc.scalar.copy(out=dst, in_=src)
 
-        def cast_q(i, engine):
-            n, a = place(q_chunks, i)
-            copy_on(engine, q_bf[:, i * QT:(i + 1) * QT, :].rearrange("p (c i) j -> p c j i", i=4),
-                    q_raw[n][:, :, a:a + QT].rearrange("p j (c i) -> p c j i", i=4))
+        def round_q(i, engine, lo=0, hi=QT):
+            n, a = place(i)
+            copy_on(engine, q_bf[:, i * QT + lo:i * QT + hi, :].rearrange("p (c i) j -> p c j i", i=4),
+                    q_raw[n][:, :, a + lo:a + hi].rearrange("p j (c i) -> p c j i", i=4))
 
-        def cast_k(s0, s1, engine):
-            part = s0 // k_span
-            src = k_raw[part][:, :, PACK * (s0 - k_span * part):PACK * (s1 - k_span * part)]
+        def round_k(s0, s1, engine):
             copy_on(engine, k_bf[:, :, s0:s1, :].rearrange("p (a b) s j -> p s a j b", b=2),
-                    src.rearrange("p j (s a b) -> p s a j b", a=2, b=2))
+                    k_raw[:, :, PACK * s0:PACK * s1].rearrange("p j (s a b) -> p s a j b", a=2, b=2))
 
-        def cast_v(h, engine):
+        def round_v(h, engine):
             copy_on(engine, v_bf[:, h, :, :].rearrange("p (c i) r -> p c r i", i=4),
                     v_raw[h][:].rearrange("p r (c i) -> p c r i", i=4))
 
@@ -119,13 +111,12 @@ def tile_rows_a_tanh_mask_onorm_kernel(tc, qT, kT, t, v, mask, gn, out):
             nc.vector.quantize_mx(out=codes.bitcast(FP8X4), scales=scales, in_=src)
 
         def quant_q(i):
-            a, b = i * QT, (i + 1) * QT
-            quantize(q_codes[:, a:b], q_scales[:, a:b], q_bf[:, a:b, :].rearrange("p q j -> p (q j)"))
+            cols = slice(i * QT, (i + 1) * QT)
+            quantize(q_codes[:, cols], q_scales[:, cols], q_bf[:, cols, :].rearrange("p q j -> p (q j)"))
 
-        def quant_k(r, part):
-            cols = slice(r * P + part * k_span, r * P + (part + 1) * k_span)
-            quantize(k_codes[:, cols], k_scales[:, cols],
-                     k_bf[:, r, part * k_span:(part + 1) * k_span, :].rearrange("p s j -> p (s j)"))
+        def quant_k(r):
+            cols = slice(r * P, (r + 1) * P)
+            quantize(k_codes[:, cols], k_scales[:, cols], k_bf[:, r, :, :].rearrange("p s j -> p (s j)"))
 
         def quant_v(h):
             cols = slice(h * E, (h + 1) * E)
@@ -134,41 +125,32 @@ def tile_rows_a_tanh_mask_onorm_kernel(tc, qT, kT, t, v, mask, gn, out):
         def quant_w(u):
             quantize(w_codes[u][:], w_scales[u][:], w_bf[u][:].rearrange("p q r -> p (q r)"))
 
-        def score(u, r):
-            i, h = divmod(u, H)
+        def score_pair(i, r):
             qc = slice(i * QT, (i + 1) * QT)
             kc = slice(r * P, (r + 1) * P)
-            rows = slice(h * ROWS, (h + 1) * ROWS)
-            nc.tensor.matmul_mx(
-                out=scores[h][i % 2][:, r, :],
-                lhsT=k_codes[rows, kc].bitcast(FP8X4), lhsT_scale=k_scales[rows, kc],
-                rhs=q_codes[rows, qc].bitcast(FP8X4), rhs_scale=q_scales[rows, qc],
-                start=True, stop=True)
-
-        def pair(i, r):
             for h in range(H):
-                score(H * i + h, r)
+                rows = slice(h * ROWS, (h + 1) * ROWS)
+                nc.tensor.matmul_mx(
+                    out=scores[h][i % 2][:, r, :],
+                    lhsT=k_codes[rows, kc].bitcast(FP8X4), lhsT_scale=k_scales[rows, kc],
+                    rhs=q_codes[rows, qc].bitcast(FP8X4), rhs_scale=q_scales[rows, qc],
+                    start=True, stop=True)
 
         def scores_of(i):
             for r in range(PACK):
-                pair(i, r)
+                score_pair(i, r)
 
         def tanh(u):
             i, h = divmod(u, H)
             nc.scalar.activation(out=p_sb[u][:], in_=scores[h][i % 2][:], func=ACT.Tanh)
 
-        def mask_t(first, engine):
-            i = place(m_chunks, first)[0]
+        def mask_times_t(n):
             for r in range(PACK):
-                src = m_raw[i][:, r, :]
-                if engine == "V":
-                    nc.vector.tensor_scalar(out=mt[i][:, r, :], in0=src, scalar1=t_sb[:, r:r + 1],
-                                            scalar2=None, op0=ALU.mult)
-                else:
-                    nc.scalar.activation(out=mt[i][:, r, :], in_=src, func=ACT.Copy, scale=t_sb[:, r:r + 1])
+                nc.vector.tensor_scalar(out=mt[n][:, r, :], in0=m_raw[n][:, r, :], scalar1=t_sb[:, r:r + 1],
+                                        scalar2=None, op0=ALU.mult)
 
         def weigh(u):
-            n, a = place(m_chunks, u // H)
+            n, a = place(u // H)
             nc.vector.tensor_tensor(
                 out=w_bf[u][:].rearrange("p (c i) r -> p c r i", i=2),
                 in0=p_sb[u][:].rearrange("p r (c i) -> p c r i", i=2),
@@ -176,8 +158,7 @@ def tile_rows_a_tanh_mask_onorm_kernel(tc, qT, kT, t, v, mask, gn, out):
                 op=ALU.mult)
 
         def product(u):
-            i, h = divmod(u, H)
-            ec = slice(h * E, (h + 1) * E)
+            ec = slice((u % H) * E, (u % H + 1) * E)
             nc.tensor.matmul_mx(
                 out=y_of(u),
                 lhsT=w_codes[u][:].bitcast(FP8X4), lhsT_scale=w_scales[u][:],
@@ -185,128 +166,110 @@ def tile_rows_a_tanh_mask_onorm_kernel(tc, qT, kT, t, v, mask, gn, out):
                 start=True, stop=True)
 
         def square(u):
-            i, h = divmod(u, H)
-            nc.scalar.activation(out=squares[:, u, :], in_=y_of(u), func=ACT.Square,
-                                 accum_out=ssq[:, u:u + 1])
+            nc.scalar.activation(out=squares[:, u, :], in_=y_of(u), func=ACT.Square, accum_out=ssq[:, u:u + 1])
 
-        def sqrt(a, b):
-            nc.scalar.activation(out=root[:, a:b], in_=ssq[:, a:b], func=ACT.Sqrt, scale=1.0 / E, bias=EPS)
-
-        def rsqrt(a, b):
-            nc.scalar.activation(out=rstd[:, a:b], in_=ssq[:, a:b], func=ACT.Abs_reciprocal_sqrt, scale=1.0 / E, bias=EPS)
-
-        def recip(a, b):
-            nc.vector.reciprocal(out=rstd[:, a:b], in_=root[:, a:b])
+        def rsqrt(first, last):
+            cols = slice(first, last + 1)
+            nc.scalar.activation(out=rstd[:, cols], in_=ssq[:, cols], func=ACT.Abs_reciprocal_sqrt,
+                                 scale=1.0 / E, bias=eps[:])
 
         def finish(u):
             i, h = divmod(u, H)
             nc.vector.scalar_tensor_tensor(out=res[i][:, h, :], in0=y_of(u), scalar=rstd[:, u:u + 1],
                                            in1=gn_sb[:], op0=ALU.mult, op1=ALU.mult)
 
+        def store_tile(i):
+            nc.sync.dma_start(out=out[:, i * QT:(i + 1) * QT, :].rearrange("h q e -> q h e"), in_=res[i][:])
+
         def store_unit(u):
             i, h = divmod(u, H)
             nc.sync.dma_start(out=out[h, i * QT:(i + 1) * QT, :], in_=res[i][:, h, :])
 
-        def store(i):
-            nc.sync.dma_start(out=out[:, i * QT:(i + 1) * QT, :].rearrange("h q e -> q h e"), in_=res[i][:])
-
-        nc.scalar.dma_start(out=t_sb[:], in_=t.rearrange("(s r) o -> s (r o)", r=PACK))
-        load_k(0)
-        load_q(0)
-        load_q(1)
-        load_q(2)
-        load_m(0)
+        nc.sync.dma_start(out=k_raw[:], in_=k_hbm)
+        load_columns(q_raw, q_hbm, 0)
+        load_columns(q_raw, q_hbm, 1)
+        nc.sync.dma_start(out=t_sb[:], in_=t.rearrange("(s r) o -> s (r o)", r=PACK))
+        load_columns(q_raw, q_hbm, 2)
+        load_columns(m_raw, m_hbm, 0)
         load_v(0)
-        load_m(1)
+        load_columns(m_raw, m_hbm, 1)
         load_v(1)
-        load_m(2)
+        load_columns(m_raw, m_hbm, 2)
         nc.sync.dma_start(out=gn_sb[:], in_=gn)
-        nc.vector.memset(warm[:, 0:1], 0.0)
-        nc.scalar.activation(out=warm[:, 1:2], in_=warm[:, 0:1], func=ACT.Tanh)
-        cast_k(0, 84, "V")
-        cast_k(84, 128, "S")
-        cast_q(0, "V")
-        quant_k(0, 0)
+
+        nc.vector.memset(zero[:], 0.0)
+        nc.scalar.activation(out=eps[:], in_=zero[:], func=ACT.Identity, bias=EPS)
+
+        round_k(0, K_VECTOR, "V")
+        round_k(K_VECTOR, P, "S")
+        round_q(0, "V", 0, Q_VECTOR)
+        round_q(0, "S", Q_VECTOR, QT)
+        quant_k(0)
         quant_q(0)
-        cast_q(1, "S")
-        quant_k(1, 0)
-        quant_k(2, 0)
-        pair(0, 0)
-        pair(0, 1)
-        quant_k(3, 0)
+        round_q(1, "S")
+        for r in range(1, PACK):
+            quant_k(r)
+        scores_of(0)
+
         quant_q(1)
-        pair(0, 2)
-        cast_q(2, "V")
-        cast_q(3, "S")
-        pair(0, 3)
+        round_q(2, "V")
+        round_q(3, "S")
         scores_of(1)
         quant_q(2)
-        mask_t(0, "V")
         tanh(0)
+        mask_times_t(0)
         quant_q(3)
         tanh(1)
-        cast_v(0, "V")
+        round_v(0, "V")
         weigh(0)
         tanh(2)
         scores_of(2)
-        mask_t(1, "V")
+        mask_times_t(1)
         tanh(3)
-        weigh(1)
-        cast_v(1, "S")
-        weigh(2)
-        scores_of(3)
-        tanh(4)
         quant_v(0)
         quant_w(0)
-        mask_t(2, "V")
-        tanh(5)
-        product(0)
+        weigh(1)
+        round_v(1, "S")
+        scores_of(3)
+        weigh(2)
+        tanh(4)
+        quant_w(1)
         quant_v(1)
+        tanh(5)
+        mask_times_t(2)
+        product(0)
+        product(1)
         tanh(6)
+        quant_w(2)
         weigh(3)
         tanh(7)
-        quant_w(1)
-        weigh(4)
-        square(0)
-        nc.scalar.activation(out=warm[:, 0:1], in_=warm[:, 1:2], func=ACT.Abs_reciprocal_sqrt, bias=1.0)
-        product(1)
-        quant_w(2)
-        quant_w(3)
-        quant_w(4)
         product(2)
-        weigh(5)
-        product(3)
-        product(4)
-        weigh(6)
-        quant_w(5)
-        weigh(7)
-        square(1)
-        product(5)
-        square(2)
-        square(3)
-        quant_w(6)
-        square(4)
-        quant_w(7)
+        weigh(4)
+        for u in range(3):
+            square(u)
         rsqrt(0, 2)
-        square(5)
-        product(6)
-        rsqrt(2, 4)
-        finish(0)
-        product(7)
-        finish(1)
-        rsqrt(4, 6)
-        finish(2)
-        square(6)
-        finish(3)
-        store(0)
-        square(7)
-        finish(4)
-        rsqrt(6, 7)
-        finish(5)
-        store(1)
-        rsqrt(7, 8)
-        store(2)
-        finish(6)
-        store_unit(6)
-        finish(7)
-        store_unit(7)
+        weigh(5)
+        for u in range(3, 6):
+            quant_w(u)
+        for u in range(3, 6):
+            product(u)
+        weigh(6)
+        weigh(7)
+
+        for u in range(3, 6):
+            square(u)
+        rsqrt(3, 5)
+        for u in range(6, UNITS):
+            quant_w(u)
+            product(u)
+        for u in range(6, UNITS):
+            square(u)
+        for u in range(6, UNITS):
+            rsqrt(u, u)
+        for i in range(TILES - 1):
+            finish(H * i)
+            finish(H * i + 1)
+            store_tile(i)
+        for u in range(6, UNITS):
+            finish(u)
+            store_unit(u)

from contextlib import ExitStack

import concourse.mybir as mybir

F32 = mybir.dt.float32
BF16 = mybir.dt.bfloat16
U32 = mybir.dt.uint32
U8 = mybir.dt.uint8
FP8X4 = mybir.dt.float8_e4m3fn_x4
ACT = mybir.ActivationFunctionType
ALU = mybir.AluOpType

H, D, NQ, N, E = 2, 256, 512, 512, 128
FLOPS = 2 * H * NQ * N * (D + E)

P = 128
PACK = 4
ROWS = D // PACK
QT = 128
TILES = NQ // QT
UNITS = TILES * H
EPS = 1e-5 * 16.0 * 16.0
LOADS = [[0], [1], [2, 3]]
K_VECTOR = 84
Q_VECTOR = 80
Y_PLACE = [(0, 0), (0, 1), (0, 2), (1, 0), (1, 1), (1, 2), (2, 0), (3, 0)]
Y_BANKS, Y_SLOTS = 4, 3


def tile_rows_a_tanh_mask_onorm_kernel(tc, qT, kT, t, v, mask, gn, out):
    nc = tc.nc
    with ExitStack() as ctx:
        sb = ctx.enter_context(tc.tile_pool(name="sb", bufs=1))
        ps = ctx.enter_context(tc.psum_pool(name="ps", bufs=1))
        ctx.enter_context(tc.manual_schedule())

        def sbuf(name, shape, dtype):
            return sb.tile(shape, dtype, name=name, align_bytes=64)

        q_hbm = qT.rearrange("h (p j) q -> (h p) j q", j=PACK)
        k_hbm = kT.rearrange("h (p j) n -> (h p) j n", j=PACK)
        m_hbm = mask.rearrange("(s r) q -> s r q", r=PACK)
        v_hbm = v.rearrange("h (s r) e -> s h r e", r=PACK)

        q_raw = [sbuf("q_raw%d" % c[0], [P, PACK, QT * len(c)], F32) for c in LOADS]
        m_raw = [sbuf("m_raw%d" % c[0], [P, PACK, QT * len(c)], F32) for c in LOADS]
        k_raw = sbuf("k_raw", [P, PACK, N], F32)
        v_raw = [sbuf("v_raw%d" % h, [P, PACK, E], F32) for h in range(H)]
        t_sb = sbuf("t_sb", [P, PACK], F32)
        gn_sb = sbuf("gn_sb", [P, E], F32)
        zero = sbuf("zero", [P, 1], F32)
        eps = sbuf("eps", [P, 1], F32)

        q_bf = sbuf("q_bf", [P, NQ, PACK], BF16)
        k_bf = sbuf("k_bf", [P, PACK, P, PACK], BF16)
        v_bf = sbuf("v_bf", [P, H, E, PACK], BF16)
        q_codes = sbuf("q_codes", [P, NQ], U32)
        q_scales = sbuf("q_scales", [P, NQ], U8)
        k_codes = sbuf("k_codes", [P, N], U32)
        k_scales = sbuf("k_scales", [P, N], U8)
        v_codes = sbuf("v_codes", [P, H * E], U32)
        v_scales = sbuf("v_scales", [P, H * E], U8)
        mt = [sbuf("mt%d" % c[0], [P, PACK, QT * len(c)], F32) for c in LOADS]
        p_sb = [sbuf("p%d" % u, [P, PACK, QT], F32) for u in range(UNITS)]
        w_bf = [sbuf("w_bf%d" % u, [P, QT, PACK], BF16) for u in range(UNITS)]
        w_codes = [sbuf("w_codes%d" % u, [P, QT], U32) for u in range(UNITS)]
        w_scales = [sbuf("w_scales%d" % u, [P, QT], U8) for u in range(UNITS)]
        squares = sbuf("squares", [P, UNITS, E], BF16)
        ssq = sbuf("ssq", [P, UNITS], F32)
        rstd = sbuf("rstd", [P, UNITS], F32)
        res = [sbuf("res%d" % i, [P, H, E], F32) for i in range(TILES)]

        scores = [[ps.tile([P, PACK, QT], F32, name="sc%d_%d" % (h, b)) for b in range(2)] for h in range(H)]
        y_ps = [ps.tile([P, Y_SLOTS, E], F32, name="y%d" % b) for b in range(Y_BANKS)]

        def y_of(u):
            bank, slot = Y_PLACE[u]
            return y_ps[bank][:, slot, :]

        def place(i):
            n = [i in c for c in LOADS].index(True)
            return n, (i - LOADS[n][0]) * QT

        def load_columns(tiles, hbm, n):
            first = LOADS[n][0] * QT
            nc.sync.dma_start(out=tiles[n][:], in_=hbm[:, :, first:first + len(LOADS[n]) * QT])

        def load_v(h):
            nc.sync.dma_start(out=v_raw[h][:], in_=v_hbm[:, h, :, :])

        def copy_on(engine, dst, src):
            if engine == "V":
                nc.vector.tensor_copy(out=dst, in_=src)
            else:
                nc.scalar.copy(out=dst, in_=src)

        def round_q(i, engine, lo=0, hi=QT):
            n, a = place(i)
            copy_on(engine, q_bf[:, i * QT + lo:i * QT + hi, :].rearrange("p (c i) j -> p c j i", i=4),
                    q_raw[n][:, :, a + lo:a + hi].rearrange("p j (c i) -> p c j i", i=4))

        def round_k(s0, s1, engine):
            copy_on(engine, k_bf[:, :, s0:s1, :].rearrange("p (a b) s j -> p s a j b", b=2),
                    k_raw[:, :, PACK * s0:PACK * s1].rearrange("p j (s a b) -> p s a j b", a=2, b=2))

        def round_v(h, engine):
            copy_on(engine, v_bf[:, h, :, :].rearrange("p (c i) r -> p c r i", i=4),
                    v_raw[h][:].rearrange("p r (c i) -> p c r i", i=4))

        def quantize(codes, scales, src):
            nc.vector.quantize_mx(out=codes.bitcast(FP8X4), scales=scales, in_=src)

        def quant_q(i):
            cols = slice(i * QT, (i + 1) * QT)
            quantize(q_codes[:, cols], q_scales[:, cols], q_bf[:, cols, :].rearrange("p q j -> p (q j)"))

        def quant_k(r):
            cols = slice(r * P, (r + 1) * P)
            quantize(k_codes[:, cols], k_scales[:, cols], k_bf[:, r, :, :].rearrange("p s j -> p (s j)"))

        def quant_v(h):
            cols = slice(h * E, (h + 1) * E)
            quantize(v_codes[:, cols], v_scales[:, cols], v_bf[:, h, :, :].rearrange("p e r -> p (e r)"))

        def quant_w(u):
            quantize(w_codes[u][:], w_scales[u][:], w_bf[u][:].rearrange("p q r -> p (q r)"))

        def score_pair(i, r):
            qc = slice(i * QT, (i + 1) * QT)
            kc = slice(r * P, (r + 1) * P)
            for h in range(H):
                rows = slice(h * ROWS, (h + 1) * ROWS)
                nc.tensor.matmul_mx(
                    out=scores[h][i % 2][:, r, :],
                    lhsT=k_codes[rows, kc].bitcast(FP8X4), lhsT_scale=k_scales[rows, kc],
                    rhs=q_codes[rows, qc].bitcast(FP8X4), rhs_scale=q_scales[rows, qc],
                    start=True, stop=True)

        def scores_of(i):
            for r in range(PACK):
                score_pair(i, r)

        def tanh(u):
            i, h = divmod(u, H)
            nc.scalar.activation(out=p_sb[u][:], in_=scores[h][i % 2][:], func=ACT.Tanh)

        def mask_times_t(n):
            for r in range(PACK):
                nc.vector.tensor_scalar(out=mt[n][:, r, :], in0=m_raw[n][:, r, :], scalar1=t_sb[:, r:r + 1],
                                        scalar2=None, op0=ALU.mult)

        def weigh(u):
            n, a = place(u // H)
            nc.vector.tensor_tensor(
                out=w_bf[u][:].rearrange("p (c i) r -> p c r i", i=2),
                in0=p_sb[u][:].rearrange("p r (c i) -> p c r i", i=2),
                in1=mt[n][:, :, a:a + QT].rearrange("p r (c i) -> p c r i", i=2),
                op=ALU.mult)

        def product(u):
            ec = slice((u % H) * E, (u % H + 1) * E)
            nc.tensor.matmul_mx(
                out=y_of(u),
                lhsT=w_codes[u][:].bitcast(FP8X4), lhsT_scale=w_scales[u][:],
                rhs=v_codes[:, ec].bitcast(FP8X4), rhs_scale=v_scales[:, ec],
                start=True, stop=True)

        def square(u):
            nc.scalar.activation(out=squares[:, u, :], in_=y_of(u), func=ACT.Square, accum_out=ssq[:, u:u + 1])

        def rsqrt(first, last):
            cols = slice(first, last + 1)
            nc.scalar.activation(out=rstd[:, cols], in_=ssq[:, cols], func=ACT.Abs_reciprocal_sqrt,
                                 scale=1.0 / E, bias=eps[:])

        def finish(u):
            i, h = divmod(u, H)
            nc.vector.scalar_tensor_tensor(out=res[i][:, h, :], in0=y_of(u), scalar=rstd[:, u:u + 1],
                                           in1=gn_sb[:], op0=ALU.mult, op1=ALU.mult)

        def store_tile(i):
            nc.sync.dma_start(out=out[:, i * QT:(i + 1) * QT, :].rearrange("h q e -> q h e"), in_=res[i][:])

        def store_unit(u):
            i, h = divmod(u, H)
            nc.sync.dma_start(out=out[h, i * QT:(i + 1) * QT, :], in_=res[i][:, h, :])

        nc.sync.dma_start(out=k_raw[:], in_=k_hbm)
        load_columns(q_raw, q_hbm, 0)
        load_columns(q_raw, q_hbm, 1)
        nc.sync.dma_start(out=t_sb[:], in_=t.rearrange("(s r) o -> s (r o)", r=PACK))
        load_columns(q_raw, q_hbm, 2)
        load_columns(m_raw, m_hbm, 0)
        load_v(0)
        load_columns(m_raw, m_hbm, 1)
        load_v(1)
        load_columns(m_raw, m_hbm, 2)
        nc.sync.dma_start(out=gn_sb[:], in_=gn)

        nc.vector.memset(zero[:], 0.0)
        nc.scalar.activation(out=eps[:], in_=zero[:], func=ACT.Identity, bias=EPS)

        round_k(0, K_VECTOR, "V")
        round_k(K_VECTOR, P, "S")
        round_q(0, "V", 0, Q_VECTOR)
        round_q(0, "S", Q_VECTOR, QT)
        quant_k(0)
        quant_q(0)
        round_q(1, "S")
        for r in range(1, PACK):
            quant_k(r)
        scores_of(0)

        quant_q(1)
        round_q(2, "V")
        round_q(3, "S")
        scores_of(1)
        quant_q(2)
        tanh(0)
        mask_times_t(0)
        quant_q(3)
        tanh(1)
        round_v(0, "V")
        weigh(0)
        tanh(2)
        scores_of(2)
        mask_times_t(1)
        tanh(3)
        quant_v(0)
        quant_w(0)
        weigh(1)
        round_v(1, "S")
        scores_of(3)
        weigh(2)
        tanh(4)
        quant_w(1)
        quant_v(1)
        tanh(5)
        mask_times_t(2)
        product(0)
        product(1)
        tanh(6)
        quant_w(2)
        weigh(3)
        tanh(7)
        product(2)
        weigh(4)
        for u in range(3):
            square(u)
        rsqrt(0, 2)
        weigh(5)
        for u in range(3, 6):
            quant_w(u)
        for u in range(3, 6):
            product(u)
        weigh(6)
        weigh(7)

        for u in range(3, 6):
            square(u)
        rsqrt(3, 5)
        for u in range(6, UNITS):
            quant_w(u)
            product(u)
        for u in range(6, UNITS):
            square(u)
        for u in range(6, UNITS):
            rsqrt(u, u)
        for i in range(TILES - 1):
            finish(H * i)
            finish(H * i + 1)
            store_tile(i)
        for u in range(6, UNITS):
            finish(u)
            store_unit(u)
